import numpy as np, ml_dtypes
CORES = [35,38,43,46]
N = 4
DEG, TK, TIMES = 4, 128, 2
MASK = [[0,1,2,3],[0,1,2,3],[0,1,2,3],[0,1,2,3]]
def setup_inputs(rng):
    return {"x": rng.standard_normal((N, 128, TK), dtype=np.float32).astype(ml_dtypes.bfloat16), "w": (rng.standard_normal((N, 128, DEG * 128), dtype=np.float32) / np.float32(np.sqrt(128 * DEG / 2))).astype(ml_dtypes.bfloat16)}
def setup_inputs_big(rng):
    d = setup_inputs(rng)
    for k in ("x",): d[k] = (d[k].astype(np.float32) * 1048576.0).astype(d[k].dtype)
    return d
def setup_inputs_small(rng):
    d = setup_inputs(rng)
    for k in ("x",): d[k] = (d[k].astype(np.float32) * (1 / 1048576.0)).astype(d[k].dtype)
    return d
def setup_inputs_apart(rng):
    d = setup_inputs(rng)
    f = (10.0 ** rng.permutation(np.linspace(-1.5, 1.5, N))).astype(np.float32).reshape(N, 1, 1)
    for k in ("x",): d[k] = (d[k].astype(np.float32) * f).astype(d[k].dtype)
    return d
def reference(x, w):
    X, W = x.astype(np.float64), w.astype(np.float64)
    h = list(X)
    for _ in range(TIMES):
        h = [np.maximum(sum(W[r][:, 128 * i:128 * i + 128].T @ h[j] for i, j in enumerate(MASK[r])), 0.0) for r in range(N)]
    return {"y": np.stack(h).astype(ml_dtypes.bfloat16)}

@@ -1,0 +1,98 @@
+from concourse.bass import DstId, RemoteDMATransfer
+from concourse.mybir import AluOpType
+
+TK = 128
+NR = 4
+K_ENG = 4
+
+SCRATCH = {
+    "ws": ("sbuf", [128, NR * 128], "bfloat16"),
+    "h0": ("sbuf", [128, NR * TK], "bfloat16"),
+    "h1": ("sbuf", [128, NR * TK], "bfloat16"),
+    "h2": ("sbuf", [128, TK], "bfloat16"),
+    "zero": ("sbuf", [128, TK], "float32"),
+    "p1": ("psum", [128, 512], "float32"),
+    "p2": ("psum", [128, 512], "float32"),
+}
+SEMAPHORES = (["xl", "wl", "z", "mm1", "mm2", "r1", "r2", "ls", "st"]
+              + ["a1_%d" % j for j in range(NR)] + ["a2_%d" % j for j in range(NR)])
+
+
+def _bits(mask):
+    return [1 << b for b in range(mask.bit_length()) if (mask >> b) & 1]
+
+
+def rank_program(g, core, T, topo):
+    r = T.rank_of(core)
+    if r is None:
+        return
+    mask_tab = T.tables["MASK"]
+    cores = T.cores
+    row = mask_tab[r]
+    dests = [q for q in range(len(cores)) if q != r and r in mask_tab[q]]
+
+    def slot(buf, j):
+        return buf[:, j * TK:(j + 1) * TK]
+
+    engines = {}
+    used = 0
+    for q in sorted(dests, key=lambda q: len(_bits(topo.mask(core, cores[q])))):
+        assert topo.may_write(core, cores[q])
+        free = [b for b in _bits(topo.mask(core, cores[q])) if not used & b]
+        pick = free[::max(1, len(free) // K_ENG)][:K_ENG]
+        engines[q] = sum(pick)
+        used |= engines[q]
+
+    def send(buf, sem_name):
+        trs = []
+        for q in dests:
+            rid, pid, _ = topo.addr(cores[q])
+            trs.append(RemoteDMATransfer(dst_ids=[DstId(rid=rid, pnc=pid)], dma_engine_mask=engines[q],
+                                         remote_sem=T.sem[sem_name], src=slot(buf, r), dst=slot(buf, r)))
+        g.remote_dma_fused(trs, local_sem=T.sem.ls)
+
+    def far(j):
+        c = cores[j]
+        return (j != r, topo.chip(c) != topo.chip(core), topo.die(c) != topo.die(core))
+
+    order = sorted(range(len(row)), key=lambda i: far(row[i]))
+
+    def matmuls(buf, psum, arr, own_sem, own_val, done):
+        seen = set()
+        last = None
+        for n, i in enumerate(order):
+            j = row[i]
+            if j not in seen:
+                seen.add(j)
+                if j == r:
+                    g.tensor.wait_ge(own_sem, own_val)
+                else:
+                    g.tensor.wait_ge(T.sem["%s_%d" % (arr, j)], K_ENG)
+            last = g.tensor.matmul(psum[:, 0:TK], T.ws[:, i * 128:(i + 1) * 128], slot(buf, j),
+                                   start=(n == 0), stop=(n == len(order) - 1))
+        last.then_inc(done, 1)
+
+    g.sync.dma_start(slot(T.h0, r), T.x[:, :]).then_inc(T.sem.xl, 16)
+    g.sync.dma_start(T.ws[:, :], T.w[:, :]).then_inc(T.sem.wl, 16)
+
+    g.vector.memset(T.zero[:, :], 0.0).then_inc(T.sem.z, 1)
+    g.vector.wait_ge(T.sem.z, 1)
+
+    g.wait_ge(T.sem.xl, 16)
+    send(T.h0, "a1_%d" % r)
+    g.tensor.wait_ge(T.sem.wl, 16)
+    matmuls(T.h0, T.p1, "a1", T.sem.xl, 16, T.sem.mm1)
+    g.vector.wait_ge(T.sem.mm1, 1)
+    g.vector.tensor_tensor(slot(T.h1, r), T.p1[:, 0:TK], T.zero[:, :], AluOpType.max).then_inc(T.sem.r1, 1)
+
+    g.wait_ge(T.sem.r1, 1)
+    send(T.h1, "a2_%d" % r)
+    matmuls(T.h1, T.p2, "a2", T.sem.r1, 1, T.sem.mm2)
+    g.vector.wait_ge(T.sem.mm2, 1)
+    g.vector.tensor_tensor(T.h2[:, :], T.p2[:, 0:TK], T.zero[:, :], AluOpType.max).then_inc(T.sem.r2, 1)
+
+    g.sync.wait_ge(T.sem.r2, 1)
+    g.sync.dma_start(T.y[:, :], T.h2[:, :]).then_inc(T.sem.st, 16)
+    g.sync.wait_ge(T.sem.st, 16)
+
+    g.wait_ge(T.sem.ls, 2 * K_ENG * len(dests))

@@ -1,98 +1,137 @@
 from concourse.bass import DstId, RemoteDMATransfer
-from concourse.mybir import AluOpType
+from concourse.mybir import AluOpType, ActivationFunctionType
 
 TK = 128
+HK = TK // 2
 NR = 4
-K_ENG = 4
 
 SCRATCH = {
+    "xd": ("dram", [128, TK], "bfloat16"),
     "ws": ("sbuf", [128, NR * 128], "bfloat16"),
+    "wm": ("sbuf", [128, NR * 128], "bfloat16"),
     "h0": ("sbuf", [128, NR * TK], "bfloat16"),
     "h1": ("sbuf", [128, NR * TK], "bfloat16"),
     "h2": ("sbuf", [128, TK], "bfloat16"),
-    "zero": ("sbuf", [128, TK], "float32"),
-    "p1": ("psum", [128, 512], "float32"),
-    "p2": ("psum", [128, 512], "float32"),
+    "p1a": ("psum", [128, 512], "float32"),
+    "p1b": ("psum", [128, 512], "float32"),
+    "pma": ("psum", [128, 512], "float32"),
+    "pmb": ("psum", [128, 512], "float32"),
+    "p2a": ("psum", [128, 512], "float32"),
+    "p2b": ("psum", [128, 512], "float32"),
 }
-SEMAPHORES = (["xl", "wl", "z", "mm1", "mm2", "r1", "r2", "ls", "st"]
+SEMAPHORES = (["xs", "xl", "wl", "wa", "m1a", "m1b", "mma", "mmb", "m2a", "m2b", "r1", "rma", "rmb", "r2", "ls", "st"]
               + ["a1_%d" % j for j in range(NR)] + ["a2_%d" % j for j in range(NR)])
 
 
-def _bits(mask):
-    return [1 << b for b in range(mask.bit_length()) if (mask >> b) & 1]
+def _count(mask):
+    return sum((mask >> b) & 1 for b in range(mask.bit_length()))
 
 
 def rank_program(g, core, T, topo):
     r = T.rank_of(core)
     if r is None:
         return
-    mask_tab = T.tables["MASK"]
+    tab = T.tables["MASK"]
     cores = T.cores
-    row = mask_tab[r]
-    dests = [q for q in range(len(cores)) if q != r and r in mask_tab[q]]
+    row = tab[r]
+    assert all(sorted(t) == list(range(len(cores))) for t in tab)
+
+    others = [q for q in range(len(cores)) if q != r]
+    near = [q for q in others if topo.chip(cores[q]) == topo.chip(core)]
+    away = [q for q in others if topo.mates(topo.chip(cores[q]), topo.chip(core))]
+    same = [q for q in away if topo.die(cores[q]) == topo.die(core)]
+    cross = [q for q in away if topo.die(cores[q]) != topo.die(core)]
+    assert len(near) == 1 and len(same) == 1 and len(cross) == 1
+    assert all(topo.may_write(core, cores[q]) for q in others)
+    peer, twin, diag = near[0], same[0], cross[0]
+
+    off = topo.mask(core, cores[twin]) & topo.mask(core, cores[diag])
+    on = topo.mask(core, cores[peer]) & ~off
+    n_off, n_on = _count(off), _count(on)
 
     def slot(buf, j):
         return buf[:, j * TK:(j + 1) * TK]
 
-    engines = {}
-    used = 0
-    for q in sorted(dests, key=lambda q: len(_bits(topo.mask(core, cores[q])))):
-        assert topo.may_write(core, cores[q])
-        free = [b for b in _bits(topo.mask(core, cores[q])) if not used & b]
-        pick = free[::max(1, len(free) // K_ENG)][:K_ENG]
-        engines[q] = sum(pick)
-        used |= engines[q]
+    def half(buf, j, b):
+        return buf[:, j * TK + b * HK:j * TK + (b + 1) * HK]
 
-    def send(buf, sem_name):
-        trs = []
-        for q in dests:
+    def tr(src, dst, qs, eng, sem):
+        ids = []
+        for q in qs:
             rid, pid, _ = topo.addr(cores[q])
-            trs.append(RemoteDMATransfer(dst_ids=[DstId(rid=rid, pnc=pid)], dma_engine_mask=engines[q],
-                                         remote_sem=T.sem[sem_name], src=slot(buf, r), dst=slot(buf, r)))
-        g.remote_dma_fused(trs, local_sem=T.sem.ls)
+            ids.append(DstId(rid=rid, pnc=pid))
+        return RemoteDMATransfer(dst_ids=ids, dma_engine_mask=eng, remote_sem=sem,
+                                 srcs=[src], dsts=[dst for _ in qs])
 
-    def far(j):
-        c = cores[j]
-        return (j != r, topo.chip(c) != topo.chip(core), topo.die(c) != topo.die(core))
+    def tile(wbuf, i):
+        return wbuf[:, i * 128:(i + 1) * 128]
 
-    order = sorted(range(len(row)), key=lambda i: far(row[i]))
+    def both(pa, pb, buf, j, first, final, sa, sb):
+        wt = tile(T.ws, row.index(j))
+        ia = g.tensor.matmul(pa[:, 0:HK], wt, half(buf, j, 0), start=first, stop=final)
+        ib = g.tensor.matmul(pb[:, 0:HK], wt, half(buf, j, 1), start=first, stop=final)
+        if final:
+            ia.then_inc(sa, 1)
+            ib.then_inc(sb, 1)
 
-    def matmuls(buf, psum, arr, own_sem, own_val, done):
-        seen = set()
-        last = None
-        for n, i in enumerate(order):
-            j = row[i]
-            if j not in seen:
-                seen.add(j)
-                if j == r:
-                    g.tensor.wait_ge(own_sem, own_val)
-                else:
-                    g.tensor.wait_ge(T.sem["%s_%d" % (arr, j)], K_ENG)
-            last = g.tensor.matmul(psum[:, 0:TK], T.ws[:, i * 128:(i + 1) * 128], slot(buf, j),
-                                   start=(n == 0), stop=(n == len(order) - 1))
-        last.then_inc(done, 1)
+    def relu(pa, pb, out_a, out_b, sa, sb, done_a, done_b):
+        g.vector.wait_ge(sa, 1)
+        g.vector.tensor_scalar(out_a, pa[:, 0:HK], 0.0, None, AluOpType.max).then_inc(done_a, 1)
+        g.scalar.wait_ge(sb, 1)
+        g.scalar.activation(out_b, pb[:, 0:HK], ActivationFunctionType.Relu).then_inc(done_b, 1)
 
-    g.sync.dma_start(slot(T.h0, r), T.x[:, :]).then_inc(T.sem.xl, 16)
+    g.sync.dma_start(T.xd[:, :], T.x[:, :]).then_inc(T.sem.xs, 16)
     g.sync.dma_start(T.ws[:, :], T.w[:, :]).then_inc(T.sem.wl, 16)
+    g.sync.dma_start(slot(T.h0, r), T.x[:, :]).then_inc(T.sem.xl, 16)
 
-    g.vector.memset(T.zero[:, :], 0.0).then_inc(T.sem.z, 1)
-    g.vector.wait_ge(T.sem.z, 1)
+    a1 = T.sem["a1_%d" % r]
+    a2 = T.sem["a2_%d" % r]
+    g.wait_ge(T.sem.xs, 16)
+    g.remote_dma_fused([tr(T.xd[:, :], slot(T.h0, r), [twin, diag], off, a1)], local_sem=T.sem.ls)
+    g.remote_dma_fused([tr(T.xd[:, :], slot(T.h0, r), [peer], on, a1)], local_sem=T.sem.ls)
+    g.wait_ge(T.sem.wl, 16)
+    g.remote_dma_fused([tr(T.ws[:, :], T.wm[:, :], [diag], off, T.sem.wa)], local_sem=T.sem.ls)
 
-    g.wait_ge(T.sem.xl, 16)
-    send(T.h0, "a1_%d" % r)
     g.tensor.wait_ge(T.sem.wl, 16)
-    matmuls(T.h0, T.p1, "a1", T.sem.xl, 16, T.sem.mm1)
-    g.vector.wait_ge(T.sem.mm1, 1)
-    g.vector.tensor_tensor(slot(T.h1, r), T.p1[:, 0:TK], T.zero[:, :], AluOpType.max).then_inc(T.sem.r1, 1)
+    g.tensor.wait_ge(T.sem.xl, 16)
+    both(T.p1a, T.p1b, T.h0, r, True, False, None, None)
+    g.tensor.wait_ge(T.sem["a1_%d" % twin], n_off)
+    both(T.p1a, T.p1b, T.h0, twin, False, False, None, None)
+    g.tensor.wait_ge(T.sem["a1_%d" % peer], n_on)
+    both(T.p1a, T.p1b, T.h0, peer, False, False, None, None)
+    g.tensor.wait_ge(T.sem["a1_%d" % diag], n_off)
+    both(T.p1a, T.p1b, T.h0, diag, False, True, T.sem.m1a, T.sem.m1b)
+    relu(T.p1a, T.p1b, half(T.h1, r, 0), half(T.h1, r, 1), T.sem.m1a, T.sem.m1b, T.sem.r1, T.sem.r1)
 
-    g.wait_ge(T.sem.r1, 1)
-    send(T.h1, "a2_%d" % r)
-    matmuls(T.h1, T.p2, "a2", T.sem.r1, 1, T.sem.mm2)
-    g.vector.wait_ge(T.sem.mm2, 1)
-    g.vector.tensor_tensor(T.h2[:, :], T.p2[:, 0:TK], T.zero[:, :], AluOpType.max).then_inc(T.sem.r2, 1)
+    g.wait_ge(T.sem.r1, 2)
+    g.remote_dma_fused([tr(slot(T.h1, r), slot(T.h1, r), [twin], off, a2),
+                        tr(slot(T.h1, r), slot(T.h1, r), [peer], on, a2)], local_sem=T.sem.ls)
 
-    g.sync.wait_ge(T.sem.r2, 1)
-    g.sync.dma_start(T.y[:, :], T.h2[:, :]).then_inc(T.sem.st, 16)
-    g.sync.wait_ge(T.sem.st, 16)
+    g.tensor.wait_ge(T.sem.r1, 2)
+    both(T.p2a, T.p2b, T.h1, r, True, False, None, None)
+    g.tensor.wait_ge(T.sem.wa, n_off)
+    n_t = len(tab[diag])
+    for b, (pbank, sem) in enumerate(((T.pma, T.sem.mma), (T.pmb, T.sem.mmb))):
+        last = None
+        for i, j in enumerate(tab[diag]):
+            last = g.tensor.matmul(pbank[:, 0:HK], tile(T.wm, i), half(T.h0, j, b),
+                                   start=(i == 0), stop=(i == n_t - 1))
+        last.then_inc(sem, 1)
+    relu(T.pma, T.pmb, half(T.h1, diag, 0), half(T.h1, diag, 1), T.sem.mma, T.sem.mmb, T.sem.rma, T.sem.rmb)
 
-    g.wait_ge(T.sem.ls, 2 * K_ENG * len(dests))
+    wd = tile(T.ws, row.index(diag))
+    g.tensor.wait_ge(T.sem.rma, 1)
+    g.tensor.matmul(T.p2a[:, 0:HK], wd, half(T.h1, diag, 0), start=False, stop=False)
+    g.tensor.wait_ge(T.sem.rmb, 1)
+    g.tensor.matmul(T.p2b[:, 0:HK], wd, half(T.h1, diag, 1), start=False, stop=False)
+    g.tensor.wait_ge(T.sem["a2_%d" % peer], n_on)
+    both(T.p2a, T.p2b, T.h1, peer, False, False, None, None)
+    g.tensor.wait_ge(T.sem["a2_%d" % twin], n_off)
+    both(T.p2a, T.p2b, T.h1, twin, False, True, T.sem.m2a, T.sem.m2b)
+    relu(T.p2a, T.p2b, T.h2[:, 0:HK], T.h2[:, HK:TK], T.sem.m2a, T.sem.m2b, T.sem.r2, T.sem.r2)
+
+    g.scalar.wait_ge(T.sem.r2, 2)
+    g.scalar.dma_start(T.y[:, :], T.h2[:, :]).then_inc(T.sem.st, 16)
+    g.scalar.wait_ge(T.sem.st, 16)
+
+    g.wait_ge(T.sem.ls, 3 * n_off + 2 * n_on)

from concourse.bass import DstId, RemoteDMATransfer
from concourse.mybir import AluOpType, ActivationFunctionType

TK = 128
HK = TK // 2
NR = 4

SCRATCH = {
    "xd": ("dram", [128, TK], "bfloat16"),
    "ws": ("sbuf", [128, NR * 128], "bfloat16"),
    "wm": ("sbuf", [128, NR * 128], "bfloat16"),
    "h0": ("sbuf", [128, NR * TK], "bfloat16"),
    "h1": ("sbuf", [128, NR * TK], "bfloat16"),
    "h2": ("sbuf", [128, TK], "bfloat16"),
    "p1a": ("psum", [128, 512], "float32"),
    "p1b": ("psum", [128, 512], "float32"),
    "pma": ("psum", [128, 512], "float32"),
    "pmb": ("psum", [128, 512], "float32"),
    "p2a": ("psum", [128, 512], "float32"),
    "p2b": ("psum", [128, 512], "float32"),
}
SEMAPHORES = (["xs", "xl", "wl", "wa", "m1a", "m1b", "mma", "mmb", "m2a", "m2b", "r1", "rma", "rmb", "r2", "ls", "st"]
              + ["a1_%d" % j for j in range(NR)] + ["a2_%d" % j for j in range(NR)])


def _count(mask):
    return sum((mask >> b) & 1 for b in range(mask.bit_length()))


def rank_program(g, core, T, topo):
    r = T.rank_of(core)
    if r is None:
        return
    tab = T.tables["MASK"]
    cores = T.cores
    row = tab[r]
    assert all(sorted(t) == list(range(len(cores))) for t in tab)

    others = [q for q in range(len(cores)) if q != r]
    near = [q for q in others if topo.chip(cores[q]) == topo.chip(core)]
    away = [q for q in others if topo.mates(topo.chip(cores[q]), topo.chip(core))]
    same = [q for q in away if topo.die(cores[q]) == topo.die(core)]
    cross = [q for q in away if topo.die(cores[q]) != topo.die(core)]
    assert len(near) == 1 and len(same) == 1 and len(cross) == 1
    assert all(topo.may_write(core, cores[q]) for q in others)
    peer, twin, diag = near[0], same[0], cross[0]

    off = topo.mask(core, cores[twin]) & topo.mask(core, cores[diag])
    on = topo.mask(core, cores[peer]) & ~off
    n_off, n_on = _count(off), _count(on)

    def slot(buf, j):
        return buf[:, j * TK:(j + 1) * TK]

    def half(buf, j, b):
        return buf[:, j * TK + b * HK:j * TK + (b + 1) * HK]

    def tr(src, dst, qs, eng, sem):
        ids = []
        for q in qs:
            rid, pid, _ = topo.addr(cores[q])
            ids.append(DstId(rid=rid, pnc=pid))
        return RemoteDMATransfer(dst_ids=ids, dma_engine_mask=eng, remote_sem=sem,
                                 srcs=[src], dsts=[dst for _ in qs])

    def tile(wbuf, i):
        return wbuf[:, i * 128:(i + 1) * 128]

    def both(pa, pb, buf, j, first, final, sa, sb):
        wt = tile(T.ws, row.index(j))
        ia = g.tensor.matmul(pa[:, 0:HK], wt, half(buf, j, 0), start=first, stop=final)
        ib = g.tensor.matmul(pb[:, 0:HK], wt, half(buf, j, 1), start=first, stop=final)
        if final:
            ia.then_inc(sa, 1)
            ib.then_inc(sb, 1)

    def relu(pa, pb, out_a, out_b, sa, sb, done_a, done_b):
        g.vector.wait_ge(sa, 1)
        g.vector.tensor_scalar(out_a, pa[:, 0:HK], 0.0, None, AluOpType.max).then_inc(done_a, 1)
        g.scalar.wait_ge(sb, 1)
        g.scalar.activation(out_b, pb[:, 0:HK], ActivationFunctionType.Relu).then_inc(done_b, 1)

    g.sync.dma_start(T.xd[:, :], T.x[:, :]).then_inc(T.sem.xs, 16)
    g.sync.dma_start(T.ws[:, :], T.w[:, :]).then_inc(T.sem.wl, 16)
    g.sync.dma_start(slot(T.h0, r), T.x[:, :]).then_inc(T.sem.xl, 16)

    a1 = T.sem["a1_%d" % r]
    a2 = T.sem["a2_%d" % r]
    g.wait_ge(T.sem.xs, 16)
    g.remote_dma_fused([tr(T.xd[:, :], slot(T.h0, r), [twin, diag], off, a1)], local_sem=T.sem.ls)
    g.remote_dma_fused([tr(T.xd[:, :], slot(T.h0, r), [peer], on, a1)], local_sem=T.sem.ls)
    g.wait_ge(T.sem.wl, 16)
    g.remote_dma_fused([tr(T.ws[:, :], T.wm[:, :], [diag], off, T.sem.wa)], local_sem=T.sem.ls)

    g.tensor.wait_ge(T.sem.wl, 16)
    g.tensor.wait_ge(T.sem.xl, 16)
    both(T.p1a, T.p1b, T.h0, r, True, False, None, None)
    g.tensor.wait_ge(T.sem["a1_%d" % twin], n_off)
    both(T.p1a, T.p1b, T.h0, twin, False, False, None, None)
    g.tensor.wait_ge(T.sem["a1_%d" % peer], n_on)
    both(T.p1a, T.p1b, T.h0, peer, False, False, None, None)
    g.tensor.wait_ge(T.sem["a1_%d" % diag], n_off)
    both(T.p1a, T.p1b, T.h0, diag, False, True, T.sem.m1a, T.sem.m1b)
    relu(T.p1a, T.p1b, half(T.h1, r, 0), half(T.h1, r, 1), T.sem.m1a, T.sem.m1b, T.sem.r1, T.sem.r1)

    g.wait_ge(T.sem.r1, 2)
    g.remote_dma_fused([tr(slot(T.h1, r), slot(T.h1, r), [twin], off, a2),
                        tr(slot(T.h1, r), slot(T.h1, r), [peer], on, a2)], local_sem=T.sem.ls)

    g.tensor.wait_ge(T.sem.r1, 2)
    both(T.p2a, T.p2b, T.h1, r, True, False, None, None)
    g.tensor.wait_ge(T.sem.wa, n_off)
    n_t = len(tab[diag])
    for b, (pbank, sem) in enumerate(((T.pma, T.sem.mma), (T.pmb, T.sem.mmb))):
        last = None
        for i, j in enumerate(tab[diag]):
            last = g.tensor.matmul(pbank[:, 0:HK], tile(T.wm, i), half(T.h0, j, b),
                                   start=(i == 0), stop=(i == n_t - 1))
        last.then_inc(sem, 1)
    relu(T.pma, T.pmb, half(T.h1, diag, 0), half(T.h1, diag, 1), T.sem.mma, T.sem.mmb, T.sem.rma, T.sem.rmb)

    wd = tile(T.ws, row.index(diag))
    g.tensor.wait_ge(T.sem.rma, 1)
    g.tensor.matmul(T.p2a[:, 0:HK], wd, half(T.h1, diag, 0), start=False, stop=False)
    g.tensor.wait_ge(T.sem.rmb, 1)
    g.tensor.matmul(T.p2b[:, 0:HK], wd, half(T.h1, diag, 1), start=False, stop=False)
    g.tensor.wait_ge(T.sem["a2_%d" % peer], n_on)
    both(T.p2a, T.p2b, T.h1, peer, False, False, None, None)
    g.tensor.wait_ge(T.sem["a2_%d" % twin], n_off)
    both(T.p2a, T.p2b, T.h1, twin, False, True, T.sem.m2a, T.sem.m2b)
    relu(T.p2a, T.p2b, T.h2[:, 0:HK], T.h2[:, HK:TK], T.sem.m2a, T.sem.m2b, T.sem.r2, T.sem.r2)

    g.scalar.wait_ge(T.sem.r2, 2)
    g.scalar.dma_start(T.y[:, :], T.h2[:, :]).then_inc(T.sem.st, 16)
    g.scalar.wait_ge(T.sem.st, 16)

    g.wait_ge(T.sem.ls, 3 * n_off + 2 * n_on)
